import numpy as np
import ml_dtypes


def mxq(x, axis, fmt="e4m3"):
    dtype, down = {"e4m3": (ml_dtypes.float8_e4m3fn, 7), "e5m2": (ml_dtypes.float8_e5m2, 14)}[fmt]
    v = np.moveaxis(np.asarray(x, np.float32).astype(ml_dtypes.bfloat16).astype(np.float64), axis, -1)
    blocks = v.reshape(v.shape[:-1] + (-1, 32))
    amax = np.abs(blocks).max(-1, keepdims=True)
    byte = np.maximum(np.where(amax > 0, np.frexp(amax)[1] - 1 + 127, 0) - down, 1)
    scale = np.exp2(byte - 127.0)
    codes = (blocks / scale).astype(np.float32).astype(dtype).astype(np.float64)
    return np.moveaxis((codes * scale).reshape(v.shape), -1, axis)


WIDE = False


def mx_kscale(k):
    if not WIDE:
        return np.ones(k)
    levels = np.array([10, -10, 5, -5, 0])
    if k % 512:
        return np.exp2(np.random.permutation(np.resize(levels, k // 32))).repeat(32)
    a = np.empty((k // 512, 16))
    for p in range(k // 512):
        a[p, :8] = np.random.permutation(np.resize(levels, 8))
        for g in range(8):
            far = levels[np.abs(levels - a[p, g]) >= 10]
            a[p, g + 8] = far[np.random.randint(len(far))]
    return np.exp2(a.ravel()).repeat(32)


def f64(x):
    return np.asarray(x).astype(np.float64)


def striped(idx):
    return np.tile(idx.reshape(-1, 16).T, (8, 1)).astype(np.uint16)


def unstriped(offs):
    return offs[:16].T.reshape(-1).astype(np.int64)


def pack_weight(w):
    k, n = w.shape
    w = f64(np.asarray(w, np.float32).astype(ml_dtypes.bfloat16)).reshape(k // 32, 32, n)
    amax = np.abs(w).max(1)
    byte = np.clip(np.where(amax > 0, np.frexp(amax)[1] - 1 + 127 - 7, 1), 1, 254)
    scaled = (w * np.exp2(127.0 - byte)[:, None, :]).reshape(k, n).astype(np.float32)
    words = np.ascontiguousarray(scaled.reshape(k // 512, 128, 4, n).transpose(0, 1, 3, 2)).astype(ml_dtypes.float8_e4m3fn).view(np.uint8)
    return words, np.ascontiguousarray(byte.astype(np.uint8).reshape(k // 512, 16, n))


def unpack_weight(words, scales):
    g, p, n, _ = words.shape
    vals = np.ascontiguousarray(words).view(ml_dtypes.float8_e4m3fn).astype(np.float64) * np.repeat(np.exp2(scales.astype(np.float64) - 127.0), 8, axis=1)[..., None]
    return vals.transpose(0, 1, 3, 2).reshape(g * 512, n)


E2M1 = np.array([0.0, 0.5, 1.0, 1.5, 2.0, 3.0, 4.0, 6.0, -0.0, -0.5, -1.0, -1.5, -2.0, -3.0, -4.0, -6.0])


def pack_fp4(w):
    k, n = w.shape
    w = f64(np.asarray(w, np.float32).astype(ml_dtypes.bfloat16)).reshape(k // 32, 32, n)
    amax = np.abs(w).max(1)
    mant, ex = np.frexp(amax / 6.0)
    byte = np.clip(np.where(amax > 0, np.where(mant > 0.5, ex, ex - 1) + 127, 1), 1, 254)
    scaled = (w * np.exp2(127.0 - byte)[:, None, :]).reshape(k, n).astype(np.float32)
    c = np.ascontiguousarray(scaled.reshape(k // 512, 128, 4, n).transpose(0, 1, 3, 2)).astype(ml_dtypes.float4_e2m1fn).view(np.uint8) & 0xF
    words = (c[..., 0::2] | (c[..., 1::2] << 4)).reshape(k // 512, 128, 2 * n)
    return np.ascontiguousarray(words), np.ascontiguousarray(byte.astype(np.uint8).reshape(k // 512, 16, n))


def unpack_fp4(words, scales):
    g, _, n = scales.shape
    words = np.ascontiguousarray(words).reshape(g, 128, n, 2)
    nib = np.empty((g, 128, n, 4), np.uint8)
    nib[..., 0::2] = words & 0xF
    nib[..., 1::2] = words >> 4
    vals = E2M1[nib] * np.repeat(np.exp2(scales.astype(np.float64) - 127.0), 8, axis=1)[..., None]
    return vals.transpose(0, 1, 3, 2).reshape(g * 512, n)


def sigmoid(v):
    return 1.0 / (1.0 + np.exp(-np.maximum(v, -700.0)))


K, T, S, N, H = 1024, 1024, 512, 256, 512


def setup_inputs():
    n = np.random.standard_normal
    s = mx_kscale(K)[:, None]
    u = mx_kscale(H)
    packed_xT = pack_weight(n((K, T)) * s)
    packed_w1 = pack_fp4(n((K, H)) / np.sqrt(K) / s)
    packed_w2 = pack_fp4(n((K, H)) / np.sqrt(K) / s)
    packed_w3 = pack_fp4(n((H, N)) / np.sqrt(H) / u[:, None])
    return {
        "x_words": packed_xT[0],
        "x_scales": packed_xT[1],
        "w1_words": packed_w1[0],
        "w1_scales": packed_w1[1],
        "w2_words": packed_w2[0],
        "w2_scales": packed_w2[1],
        "unit": (np.random.uniform(0.6, 1.4, (H, 1)) * u[:, None]).astype(np.float32),
        "w3_words": packed_w3[0],
        "w3_scales": packed_w3[1],
        "offs": striped(np.random.permutation(T)[:S]),
        "s1": striped(np.random.permutation(S)),
        "s2": striped(np.random.permutation(S)),
        "far": striped(np.random.permutation(S)),
    }


def reference(x_words, x_scales, w1_words, w1_scales, w2_words, w2_scales, unit, w3_words, w3_scales, offs, s1, s2, far):
    xq = unpack_weight(x_words, x_scales)[:, unstriped(offs)]
    ys = unpack_fp4(w2_words, w2_scales).T @ xq
    crest = sigmoid(ys)
    y = unpack_fp4(w1_words, w1_scales).T @ xq
    inten = np.exp(0.8 * np.tanh(y))
    ia = inten[:, unstriped(s1)]
    ib = inten[:, unstriped(s2)]
    sur = 0.5 * (ia + ib)
    r1 = np.log(inten) - np.log(sur)
    if_ = inten[:, unstriped(far)]
    r2 = np.log(inten) - np.log(if_)
    msr = crest * r1 + (-1.0 * crest + 1.0) * r2
    rf = r1[:, unstriped(far)]
    hid = f64(unit) * (np.maximum(msr, 0.5 * rf) * inten)
    return unpack_fp4(w3_words, w3_scales).T @ mxq(hid, 0, "e4m3")

@@ -1,0 +1,196 @@
+from contextlib import ExitStack
+
+import concourse.mybir as mybir
+
+K, T, S, N, H = 1024, 1024, 512, 256, 512
+FLOPS = 2 * 2 * K * H * S + 2 * H * N * S
+
+F32 = mybir.dt.float32
+BF16 = mybir.dt.bfloat16
+I32 = mybir.dt.int32
+U32 = mybir.dt.uint32
+U16 = mybir.dt.uint16
+U8 = mybir.dt.uint8
+FP8X4 = mybir.dt.float8_e4m3fn_x4
+FP4X4 = mybir.dt.float4_e2m1fn_x4
+ALU = mybir.AluOpType
+ACT = mybir.ActivationFunctionType
+
+P = 128
+PACK = 4
+PASSES = K // (P * PACK)
+CHUNKS = (256, 256)
+
+
+def tile_picked_yretnx_max_p_kernel(
+    tc, x_words, x_scales, w1_words, w1_scales, w2_words, w2_scales, unit, w3_words, w3_scales, offs, s1, s2, far, out
+):
+    nc = tc.nc
+    with ExitStack() as ctx:
+        keep = ctx.enter_context(tc.tile_pool(name="keep", bufs=1))
+        psum = ctx.enter_context(tc.psum_pool(name="psum", bufs=1))
+
+        def load_scale_rows(tile, scales):
+            for q in range(4):
+                nc.sync.dma_start(
+                    out=tile[32 * q : 32 * q + 4, :, :].bitcast(I32),
+                    in_=scales[:, 4 * q : 4 * q + 4, :].rearrange("o r n -> r o n").bitcast(I32),
+                )
+
+        def load_list(name, source):
+            tile = keep.tile([P, S // 16], U16, name=name)
+            nc.sync.dma_start(tile[:], source)
+            return tile
+
+        def load_words(name, words):
+            tile = keep.tile([P, words.shape[0], words.shape[2]], U8, name=name, align_bytes=64)
+            nc.sync.dma_start(out=tile[:].bitcast(I32), in_=words.rearrange("o p n -> p o n").bitcast(I32))
+            return tile
+
+        xs_all = keep.tile([P, PASSES, T], U8, align_bytes=64)
+        w1s_raw = keep.tile([P, PASSES, H], U8, align_bytes=64)
+        w2s_raw = keep.tile([P, PASSES, H], U8, align_bytes=64)
+        w3s = keep.tile([P, 1, N], U8, align_bytes=64)
+        nc.vector.memset(xs_all[:].bitcast(I32), 0)
+        nc.gpsimd.memset(w1s_raw[:].bitcast(I32), 0)
+        nc.gpsimd.memset(w2s_raw[:].bitcast(I32), 0)
+        nc.gpsimd.memset(w3s[:].bitcast(I32), 0)
+
+        unit_sb = keep.tile([P, PACK], F32)
+        nc.gpsimd.dma_start(out=unit_sb[:], in_=unit.rearrange("(p t) o -> p (t o)", t=PACK))
+
+        offs_sb = load_list("offs_sb", offs)
+        xw_all = [keep.tile([P, T], I32, name=f"xw_all{o}") for o in range(PASSES)]
+        nc.sync.dma_start(out=xw_all[0][:], in_=x_words[0].rearrange("p n t -> p (n t)").bitcast(I32))
+        load_scale_rows(xs_all, x_scales)
+        nc.sync.dma_start(out=xw_all[1][:], in_=x_words[1].rearrange("p n t -> p (n t)").bitcast(I32))
+        w1w_raw = load_words("w1w_raw", w1_words)
+        load_scale_rows(w1s_raw, w1_scales)
+        s1_sb = load_list("s1_sb", s1)
+        w2w_raw = load_words("w2w_raw", w2_words)
+        load_scale_rows(w2s_raw, w2_scales)
+        s2_sb = load_list("s2_sb", s2)
+        far_sb = load_list("far_sb", far)
+        w3w = load_words("w3w", w3_words)
+        load_scale_rows(w3s, w3_scales)
+
+        half_unit = keep.tile([P, PACK], F32)
+        nc.scalar.activation(out=half_unit[:], in_=unit_sb[:], func=ACT.Copy, scale=0.5)
+
+        xs = [keep.tile([P, S], U8, name=f"xs{o}", align_bytes=64) for o in range(PASSES)]
+        xw = [keep.tile([P, S], U32, name=f"xw{o}", align_bytes=64) for o in range(PASSES)]
+        for o in range(PASSES):
+            nc.vector.tensor_copy(xs[o][:], xs_all[:, o, :].indirect(offs_sb[:]))
+
+        def deal(name, words_raw, scales_raw):
+            words = keep.tile([P, PASSES, 2 * H], U8, name=name + "w", tag=name + "w", align_bytes=64)
+            scales = keep.tile([P, PASSES, H], U8, name=name + "s", tag=name + "s", align_bytes=64)
+            for o in range(PASSES):
+                nc.scalar.copy(
+                    out=words[:, o, :].bitcast(U16).rearrange("p (t m) -> p t m", t=PACK),
+                    in_=words_raw[:, o, :].bitcast(U16).rearrange("p (m t) -> p t m", t=PACK),
+                )
+            nc.vector.tensor_copy(
+                out=scales[:].rearrange("p o (t m) -> p o t m", t=PACK),
+                in_=scales_raw[:].rearrange("p o (m t) -> p o t m", t=PACK),
+            )
+            return words, scales
+
+        nc.vector.tensor_copy(xw[0][:], xw_all[0][:].bitcast(U32).indirect(offs_sb[:]))
+        w1w, w1s = deal("w1", w1w_raw, w1s_raw)
+        nc.vector.tensor_copy(xw[1][:], xw_all[1][:].bitcast(U32).indirect(offs_sb[:]))
+        w2w, w2s = deal("w2", w2w_raw, w2s_raw)
+
+        def product(words, scales, t, bank):
+            acc = psum.tile([P, S], F32, name=f"acc{bank}", tag=f"bank{bank}")
+            for o in range(PASSES):
+                nc.tensor.matmul_mx(
+                    out=acc[:],
+                    lhsT=words[:, o, 2 * P * t : 2 * P * (t + 1)].bitcast(FP4X4),
+                    lhsT_scale=scales[:, o, P * t : P * (t + 1)],
+                    rhs=xw[o][:].bitcast(FP8X4),
+                    rhs_scale=xs[o][:],
+                    start=(o == 0),
+                    stop=(o == PASSES - 1),
+                )
+            return acc
+
+        def rows(name, dtype=F32):
+            return [keep.tile([P, S], dtype, name=f"{name}{t}") for t in range(PACK)]
+
+        tanh_y, inten, near1, tanh_ys, r1, r1_far = (rows(n) for n in ("tanh_y", "inten", "near1", "tanh_ys", "r1", "r1_far"))
+        for t in range(PACK):
+            y = product(w1w, w1s, t, t)
+            nc.scalar.activation(out=tanh_y[t][:], in_=y[:], func=ACT.Tanh)
+            nc.scalar.activation(out=inten[t][:], in_=tanh_y[t][:], func=ACT.Exp, scale=0.8)
+        for t in range(PACK):
+            ys = product(w2w, w2s, t, PACK + t)
+            nc.scalar.activation(out=tanh_ys[t][:], in_=ys[:], func=ACT.Tanh, scale=0.5)
+
+        half = S // 2
+        for t in range(PACK):
+            for a in range(0, S, half):
+                nc.vector.tensor_copy(near1[t][:, a : a + half], inten[t][:].indirect(s1_sb[:, a // 16 : (a + half) // 16]))
+        log_sur = keep.tile([P, PACK, S], F32, tag="w2w", align_bytes=64)
+        for t in range(PACK):
+            for a in range(0, S, half):
+                nc.vector.tensor_tensor(
+                    log_sur[:, t, a : a + half],
+                    inten[t][:].indirect(s2_sb[:, a // 16 : (a + half) // 16]),
+                    near1[t][:, a : a + half],
+                    ALU.add,
+                )
+        for t in range(PACK):
+            nc.scalar.activation(out=log_sur[:, t, :], in_=log_sur[:, t, :], func=ACT.Ln, scale=0.5)
+        for t in range(PACK):
+            nc.vector.scalar_tensor_tensor(r1[t][:], tanh_y[t][:], 0.8, log_sur[:, t, :], ALU.mult, ALU.subtract)
+
+        mix = keep.tile([P, PACK, S], F32, tag="w2s", align_bytes=64)
+        hid = keep.tile([P, PACK, S], BF16)
+        a = 0
+        for c, n in enumerate(CHUNKS):
+            cols = slice(a, a + n)
+            far_c = far_sb[:, a // 16 : (a + n) // 16]
+            for t in range(PACK):
+                nc.scalar.activation(out=mix[:, t, cols], in_=tanh_y[t][:].indirect(far_c), func=ACT.Copy)
+            for t in range(PACK):
+                nc.scalar.activation(out=r1_far[t][:, cols], in_=r1[t][:].indirect(far_c), func=ACT.Copy)
+            for t in range(PACK):
+                nc.vector.scalar_tensor_tensor(mix[:, t, cols], mix[:, t, cols], 0.8, log_sur[:, t, cols], ALU.mult, ALU.subtract)
+            for t in range(PACK):
+                nc.vector.scalar_tensor_tensor(mix[:, t, cols], tanh_ys[t][:, cols], -1.0, mix[:, t, cols], ALU.add, ALU.mult)
+            for t in range(PACK):
+                nc.vector.scalar_tensor_tensor(mix[:, t, cols], r1[t][:, cols], 2.0, mix[:, t, cols], ALU.mult, ALU.add)
+            for t in range(PACK):
+                nc.vector.tensor_tensor(mix[:, t, cols], mix[:, t, cols], r1_far[t][:, cols], ALU.max)
+            for t in range(PACK):
+                nc.vector.scalar_tensor_tensor(hid[:, t, cols], mix[:, t, cols], half_unit[:, t : t + 1], inten[t][:, cols], ALU.mult, ALU.mult)
+
+            woven = keep.tile([P, n * PACK], BF16, name=f"woven{c}", align_bytes=64)
+            weave_out = woven[:].rearrange("p (c i t) -> p c t i", i=4, t=PACK)
+            weave_in = hid[:, :, cols].rearrange("p t (c i) -> p c t i", i=4)
+            if c == len(CHUNKS) - 1:
+                nc.vector.tensor_copy(out=weave_out, in_=weave_in)
+            else:
+                nc.scalar.copy(out=weave_out, in_=weave_in)
+            hid_w = keep.tile([P, n], U32, name=f"hid_w{c}", align_bytes=64)
+            hid_s = keep.tile([P, n], U8, name=f"hid_s{c}", align_bytes=64)
+            nc.vector.quantize_mx(out=hid_w[:].bitcast(FP8X4), scales=hid_s[:], in_=woven[:])
+            for m in range(N // P):
+                acc = psum.tile([P, n], F32, name=f"out{c}_{m}", tag=f"bank{2 * c + m}")
+                nc.tensor.matmul_mx(
+                    out=acc[:],
+                    lhsT=w3w[:, 0, 2 * P * m : 2 * P * (m + 1)].bitcast(FP4X4),
+                    lhsT_scale=w3s[:, 0, P * m : P * (m + 1)],
+                    rhs=hid_w[:].bitcast(FP8X4),
+                    rhs_scale=hid_s[:],
+                    start=True,
+                    stop=True,
+                )
+                result = keep.tile([P, n], F32, name=f"result{c}_{m}")
+                if c == len(CHUNKS) - 1 and m == 1:
+                    nc.vector.tensor_copy(out=result[:], in_=acc[:])
+                else:
+                    nc.scalar.copy(out=result[:], in_=acc[:])
+                nc.sync.dma_start(out=out[P * m : P * (m + 1), cols], in_=result[:])
+            a += n

@@ -19,7 +19,7 @@ ACT = mybir.ActivationFunctionType
 P = 128
 PACK = 4
 PASSES = K // (P * PACK)
-CHUNKS = (256, 256)
+TAIL = 128
 
 
 def tile_picked_yretnx_max_p_kernel(
@@ -51,23 +51,23 @@ def tile_picked_yretnx_max_p_kernel(
         w1s_raw = keep.tile([P, PASSES, H], U8, align_bytes=64)
         w2s_raw = keep.tile([P, PASSES, H], U8, align_bytes=64)
         w3s = keep.tile([P, 1, N], U8, align_bytes=64)
-        nc.vector.memset(xs_all[:].bitcast(I32), 0)
-        nc.gpsimd.memset(w1s_raw[:].bitcast(I32), 0)
-        nc.gpsimd.memset(w2s_raw[:].bitcast(I32), 0)
-        nc.gpsimd.memset(w3s[:].bitcast(I32), 0)
+        nc.gpsimd.memset(xs_all[:].bitcast(I32), 0)
+        nc.vector.memset(w1s_raw[:].bitcast(I32), 0)
+        nc.vector.memset(w2s_raw[:].bitcast(I32), 0)
+        nc.vector.memset(w3s[:].bitcast(I32), 0)
 
         unit_sb = keep.tile([P, PACK], F32)
         nc.gpsimd.dma_start(out=unit_sb[:], in_=unit.rearrange("(p t) o -> p (t o)", t=PACK))
 
         offs_sb = load_list("offs_sb", offs)
-        xw_all = [keep.tile([P, T], I32, name=f"xw_all{o}") for o in range(PASSES)]
-        nc.sync.dma_start(out=xw_all[0][:], in_=x_words[0].rearrange("p n t -> p (n t)").bitcast(I32))
         load_scale_rows(xs_all, x_scales)
-        nc.sync.dma_start(out=xw_all[1][:], in_=x_words[1].rearrange("p n t -> p (n t)").bitcast(I32))
+        xw_all = [keep.tile([P, T], I32, name=f"xw_all{o}", tag=f"slot{o}", align_bytes=64) for o in range(PASSES)]
+        nc.sync.dma_start(out=xw_all[0][:], in_=x_words[0].rearrange("p n t -> p (n t)").bitcast(I32))
         w1w_raw = load_words("w1w_raw", w1_words)
         load_scale_rows(w1s_raw, w1_scales)
-        s1_sb = load_list("s1_sb", s1)
+        nc.sync.dma_start(out=xw_all[1][:], in_=x_words[1].rearrange("p n t -> p (n t)").bitcast(I32))
         w2w_raw = load_words("w2w_raw", w2_words)
+        s1_sb = load_list("s1_sb", s1)
         load_scale_rows(w2s_raw, w2_scales)
         s2_sb = load_list("s2_sb", s2)
         far_sb = load_list("far_sb", far)
@@ -77,120 +77,207 @@ def tile_picked_yretnx_max_p_kernel(
         half_unit = keep.tile([P, PACK], F32)
         nc.scalar.activation(out=half_unit[:], in_=unit_sb[:], func=ACT.Copy, scale=0.5)
 
+        def deal_words(name, raw):
+            dealt = []
+            for t in range(PACK):
+                tile = keep.tile([P, PASSES, 2 * P], U8, name=f"{name}{t}", tag=f"{name}{t}", align_bytes=64)
+                nc.scalar.copy(
+                    out=tile[:].bitcast(U16),
+                    in_=raw[:].bitcast(U16).rearrange("p o (m t) -> p o t m", t=PACK)[:, :, t, :],
+                )
+                dealt.append(tile)
+            return dealt
+
+        def deal_scales(dealt, raw, ts):
+            nc.vector.tensor_copy(out=dealt, in_=raw[:].rearrange("p o (m t) -> p o t m", t=PACK)[:, :, ts, :])
+
+        early = keep.tile([P, PASSES, 1, P], U8, align_bytes=64)
+        w1w = deal_words("w1w", w1w_raw)
+        w2w = deal_words("w2w", w2w_raw)
+
+        half = S // 2
         xs = [keep.tile([P, S], U8, name=f"xs{o}", align_bytes=64) for o in range(PASSES)]
         xw = [keep.tile([P, S], U32, name=f"xw{o}", align_bytes=64) for o in range(PASSES)]
         for o in range(PASSES):
             nc.vector.tensor_copy(xs[o][:], xs_all[:, o, :].indirect(offs_sb[:]))
-
-        def deal(name, words_raw, scales_raw):
-            words = keep.tile([P, PASSES, 2 * H], U8, name=name + "w", tag=name + "w", align_bytes=64)
-            scales = keep.tile([P, PASSES, H], U8, name=name + "s", tag=name + "s", align_bytes=64)
-            for o in range(PASSES):
-                nc.scalar.copy(
-                    out=words[:, o, :].bitcast(U16).rearrange("p (t m) -> p t m", t=PACK),
-                    in_=words_raw[:, o, :].bitcast(U16).rearrange("p (m t) -> p t m", t=PACK),
-                )
-            nc.vector.tensor_copy(
-                out=scales[:].rearrange("p o (t m) -> p o t m", t=PACK),
-                in_=scales_raw[:].rearrange("p o (m t) -> p o t m", t=PACK),
-            )
-            return words, scales
-
         nc.vector.tensor_copy(xw[0][:], xw_all[0][:].bitcast(U32).indirect(offs_sb[:]))
-        w1w, w1s = deal("w1", w1w_raw, w1s_raw)
-        nc.vector.tensor_copy(xw[1][:], xw_all[1][:].bitcast(U32).indirect(offs_sb[:]))
-        w2w, w2s = deal("w2", w2w_raw, w2s_raw)
+        deal_scales(early[:], w1s_raw, slice(0, 1))
+        for a in (0, half):
+            nc.vector.tensor_copy(xw[1][:, a : a + half], xw_all[1][:].bitcast(U32).indirect(offs_sb[:, a // 16 : (a + half) // 16]))
+        late = keep.tile([P, PASSES, 2 * PACK - 1, P], U8, tag="slot1", align_bytes=64)
+        deal_scales(late[:, :, : PACK - 1, :], w1s_raw, slice(1, PACK))
+        deal_scales(late[:, :, PACK - 1 :, :], w2s_raw, slice(0, PACK))
+        w1s = [[early[:, o, 0, :] if t == 0 else late[:, o, t - 1, :] for t in range(PACK)] for o in range(PASSES)]
+        w2s = [[late[:, o, PACK - 1 + t, :] for t in range(PACK)] for o in range(PASSES)]
 
-        def product(words, scales, t, bank):
-            acc = psum.tile([P, S], F32, name=f"acc{bank}", tag=f"bank{bank}")
+        banks = []
+
+        def product(words, scales, t, cols):
+            bank = len(banks) % 8
+            acc = psum.tile([P, cols.stop - cols.start], F32, name=f"acc{len(banks)}", tag=f"bank{bank}")
+            banks.append(acc)
             for o in range(PASSES):
                 nc.tensor.matmul_mx(
                     out=acc[:],
-                    lhsT=words[:, o, 2 * P * t : 2 * P * (t + 1)].bitcast(FP4X4),
-                    lhsT_scale=scales[:, o, P * t : P * (t + 1)],
-                    rhs=xw[o][:].bitcast(FP8X4),
-                    rhs_scale=xs[o][:],
+                    lhsT=words[t][:, o, :].bitcast(FP4X4),
+                    lhsT_scale=scales[o][t],
+                    rhs=xw[o][:, cols].bitcast(FP8X4),
+                    rhs_scale=xs[o][:, cols],
                     start=(o == 0),
                     stop=(o == PASSES - 1),
                 )
             return acc
 
-        def rows(name, dtype=F32):
-            return [keep.tile([P, S], dtype, name=f"{name}{t}") for t in range(PACK)]
+        both = [keep.tile([P, 2 * S], F32, name=f"both{t}") for t in range(PACK)]
+        inten = [b[:, :S] for b in both]
+        tanh_y = [b[:, S:] for b in both]
+        tanh_ys = keep.tile([P, PACK, S], F32)
 
-        tanh_y, inten, near1, tanh_ys, r1, r1_far = (rows(n) for n in ("tanh_y", "inten", "near1", "tanh_ys", "r1", "r1_far"))
-        for t in range(PACK):
-            y = product(w1w, w1s, t, t)
-            nc.scalar.activation(out=tanh_y[t][:], in_=y[:], func=ACT.Tanh)
-            nc.scalar.activation(out=inten[t][:], in_=tanh_y[t][:], func=ACT.Exp, scale=0.8)
-        for t in range(PACK):
-            ys = product(w2w, w2s, t, PACK + t)
-            nc.scalar.activation(out=tanh_ys[t][:], in_=ys[:], func=ACT.Tanh, scale=0.5)
+        def mixing_signal(t):
+            ys = product(w2w, w2s, t, slice(0, S))
+            nc.scalar.activation(out=tanh_ys[:, t, :], in_=ys[:], func=ACT.Tanh, scale=0.5)
 
-        half = S // 2
         for t in range(PACK):
-            for a in range(0, S, half):
-                nc.vector.tensor_copy(near1[t][:, a : a + half], inten[t][:].indirect(s1_sb[:, a // 16 : (a + half) // 16]))
-        log_sur = keep.tile([P, PACK, S], F32, tag="w2w", align_bytes=64)
-        for t in range(PACK):
-            for a in range(0, S, half):
-                nc.vector.tensor_tensor(
-                    log_sur[:, t, a : a + half],
-                    inten[t][:].indirect(s2_sb[:, a // 16 : (a + half) // 16]),
-                    near1[t][:, a : a + half],
-                    ALU.add,
-                )
-        for t in range(PACK):
-            nc.scalar.activation(out=log_sur[:, t, :], in_=log_sur[:, t, :], func=ACT.Ln, scale=0.5)
-        for t in range(PACK):
-            nc.vector.scalar_tensor_tensor(r1[t][:], tanh_y[t][:], 0.8, log_sur[:, t, :], ALU.mult, ALU.subtract)
+            for cols in ((slice(0, half), slice(half, S)) if t == 0 else (slice(0, S),)):
+                y = product(w1w, w1s, t, cols)
+                nc.scalar.activation(out=tanh_y[t][:, cols], in_=y[:], func=ACT.Tanh)
+                nc.scalar.activation(out=inten[t][:, cols], in_=tanh_y[t][:, cols], func=ACT.Exp, scale=0.8)
+            if t > 0:
+                mixing_signal(t - 1)
+        mixing_signal(PACK - 1)
 
-        mix = keep.tile([P, PACK, S], F32, tag="w2s", align_bytes=64)
+        near1 = keep.tile([P, PACK, S], F32)
+        near_sum = [keep.tile([P, S], F32, name=f"near_sum{t}", tag=f"w2w{t + 1}" if t in (1, 2) else f"near_sum{t}", align_bytes=64) for t in range(PACK)]
+
+        def fetch_near(t, cols):
+            nc.vector.tensor_copy(near1[:, t, cols], both[t][:].indirect(s1_sb[:, cols.start // 16 : cols.stop // 16]))
+
+        def add_near(t, cols):
+            picked = both[t][:].indirect(s2_sb[:, cols.start // 16 : cols.stop // 16])
+            nc.vector.tensor_tensor(near_sum[t][:, cols], picked, near1[:, t, cols], ALU.add)
+
+        for step in (fetch_near, add_near):
+            for cols in (slice(0, half), slice(half, S)):
+                step(0, cols)
+        fetch_near(1, slice(0, S))
+        for t in range(1, PACK):
+            if t + 1 < PACK:
+                fetch_near(t + 1, slice(0, S))
+            add_near(t, slice(0, S))
+        logs = keep.tile([P, 3 * PACK * S], F32, tag="slot1", align_bytes=64)
+        r1 = logs[:, : PACK * S].rearrange("p (t j) -> p t j", t=PACK)
+        log_sur = logs[:, PACK * S : 2 * PACK * S].rearrange("p (t j) -> p t j", t=PACK)
+
+        mix = logs[:, 2 * PACK * S :].rearrange("p (t j) -> p t j", t=PACK)
+        r1_far = keep.tile([P, PACK, S], F32)
         hid = keep.tile([P, PACK, S], BF16)
-        a = 0
-        for c, n in enumerate(CHUNKS):
-            cols = slice(a, a + n)
-            far_c = far_sb[:, a // 16 : (a + n) // 16]
-            for t in range(PACK):
-                nc.scalar.activation(out=mix[:, t, cols], in_=tanh_y[t][:].indirect(far_c), func=ACT.Copy)
-            for t in range(PACK):
-                nc.scalar.activation(out=r1_far[t][:, cols], in_=r1[t][:].indirect(far_c), func=ACT.Copy)
-            for t in range(PACK):
-                nc.vector.scalar_tensor_tensor(mix[:, t, cols], mix[:, t, cols], 0.8, log_sur[:, t, cols], ALU.mult, ALU.subtract)
-            for t in range(PACK):
-                nc.vector.scalar_tensor_tensor(mix[:, t, cols], tanh_ys[t][:, cols], -1.0, mix[:, t, cols], ALU.add, ALU.mult)
-            for t in range(PACK):
-                nc.vector.scalar_tensor_tensor(mix[:, t, cols], r1[t][:, cols], 2.0, mix[:, t, cols], ALU.mult, ALU.add)
-            for t in range(PACK):
-                nc.vector.tensor_tensor(mix[:, t, cols], mix[:, t, cols], r1_far[t][:, cols], ALU.max)
-            for t in range(PACK):
+
+        def far_slice(a, b):
+            return far_sb[:, a // 16 : b // 16]
+
+        def log_of_surround(t):
+            nc.scalar.activation(out=log_sur[:, t, :], in_=near_sum[t][:], func=ACT.Ln, scale=0.5)
+
+        def near_ratio(t):
+            nc.vector.scalar_tensor_tensor(r1[:, t, :], tanh_y[t], 0.8, log_sur[:, t, :], ALU.mult, ALU.subtract)
+
+        def fetch_tanh(t, cols):
+            for a in range(cols.start, cols.stop, half):
+                b = min(a + half, cols.stop)
+                nc.scalar.activation(out=mix[:, t, a:b], in_=tanh_y[t].indirect(far_slice(a, b)), func=ACT.Copy)
+
+        def fetch_r1(t, cols):
+            window = logs[:, t * S : (t + 2) * S]
+            nc.scalar.activation(out=r1_far[:, t, cols], in_=window.indirect(far_slice(cols.start, cols.stop)), func=ACT.Copy)
+
+        def step_e(ts, cols):
+            nc.vector.scalar_tensor_tensor(mix[:, ts, cols], mix[:, ts, cols], 0.8, log_sur[:, ts, cols], ALU.mult, ALU.subtract)
+
+        def step_g(ts, cols):
+            nc.vector.scalar_tensor_tensor(mix[:, ts, cols], tanh_ys[:, ts, cols], -1.0, mix[:, ts, cols], ALU.add, ALU.mult)
+
+        def step_m(ts, cols):
+            nc.vector.scalar_tensor_tensor(mix[:, ts, cols], r1[:, ts, cols], 2.0, mix[:, ts, cols], ALU.mult, ALU.add)
+
+        def step_x(ts, cols):
+            nc.vector.tensor_tensor(mix[:, ts, cols], mix[:, ts, cols], r1_far[:, ts, cols], ALU.max)
+
+        def step_hid(ts, cols):
+            for t in range(ts.start, ts.stop):
                 nc.vector.scalar_tensor_tensor(hid[:, t, cols], mix[:, t, cols], half_unit[:, t : t + 1], inten[t][:, cols], ALU.mult, ALU.mult)
 
+        def weave(c, cols, on_vector):
+            n = cols.stop - cols.start
             woven = keep.tile([P, n * PACK], BF16, name=f"woven{c}", align_bytes=64)
             weave_out = woven[:].rearrange("p (c i t) -> p c t i", i=4, t=PACK)
             weave_in = hid[:, :, cols].rearrange("p t (c i) -> p c t i", i=4)
-            if c == len(CHUNKS) - 1:
+            if on_vector:
                 nc.vector.tensor_copy(out=weave_out, in_=weave_in)
             else:
                 nc.scalar.copy(out=weave_out, in_=weave_in)
+            return woven
+
+        def finish(c, cols, woven, share):
+            n = cols.stop - cols.start
             hid_w = keep.tile([P, n], U32, name=f"hid_w{c}", align_bytes=64)
             hid_s = keep.tile([P, n], U8, name=f"hid_s{c}", align_bytes=64)
             nc.vector.quantize_mx(out=hid_w[:].bitcast(FP8X4), scales=hid_s[:], in_=woven[:])
+            result = keep.tile([P, N // P, n], F32, name=f"result{c}")
             for m in range(N // P):
-                acc = psum.tile([P, n], F32, name=f"out{c}_{m}", tag=f"bank{2 * c + m}")
-                nc.tensor.matmul_mx(
-                    out=acc[:],
-                    lhsT=w3w[:, 0, 2 * P * m : 2 * P * (m + 1)].bitcast(FP4X4),
-                    lhsT_scale=w3s[:, 0, P * m : P * (m + 1)],
-                    rhs=hid_w[:].bitcast(FP8X4),
-                    rhs_scale=hid_s[:],
-                    start=True,
-                    stop=True,
-                )
-                result = keep.tile([P, n], F32, name=f"result{c}_{m}")
-                if c == len(CHUNKS) - 1 and m == 1:
-                    nc.vector.tensor_copy(out=result[:], in_=acc[:])
+                acc = psum.tile([P, n], F32, name=f"out{c}_{m}", tag=f"bank{1 + 2 * c + m}")
+                for a in range(0, n, half):
+                    b = min(a + half, n)
+                    nc.tensor.matmul_mx(
+                        out=acc[:, a:b],
+                        lhsT=w3w[:, 0, 2 * P * m : 2 * P * (m + 1)].bitcast(FP4X4),
+                        lhsT_scale=w3s[:, 0, P * m : P * (m + 1)],
+                        rhs=hid_w[:, a:b].bitcast(FP8X4),
+                        rhs_scale=hid_s[:, a:b],
+                        start=True,
+                        stop=True,
+                    )
+                if share and m == 1:
+                    nc.vector.tensor_copy(out=result[:, m, :], in_=acc[:])
                 else:
-                    nc.scalar.copy(out=result[:], in_=acc[:])
-                nc.sync.dma_start(out=out[P * m : P * (m + 1), cols], in_=result[:])
-            a += n
+                    nc.scalar.copy(out=result[:, m, :], in_=acc[:])
+            nc.sync.dma_start(out=out[:, cols].rearrange("(m p) n -> p m n", p=P), in_=result[:])
+
+        first, last = slice(0, S - TAIL), slice(S - TAIL, S)
+        low, high = slice(0, 2), slice(2, 4)
+
+        log_of_surround(0)
+        log_of_surround(1)
+        fetch_tanh(0, first)
+        log_of_surround(2)
+        fetch_tanh(1, first)
+        log_of_surround(3)
+        for t in range(3):
+            near_ratio(t)
+        step_e(low, first)
+        near_ratio(3)
+        fetch_tanh(2, first)
+        fetch_tanh(3, first)
+        for t in range(PACK):
+            fetch_r1(t, first)
+        step_g(low, first)
+        step_e(high, first)
+        step_m(low, first)
+        step_g(high, first)
+        step_x(low, first)
+        step_m(high, first)
+        step_hid(low, first)
+        step_x(high, first)
+        for t in range(PACK):
+            fetch_tanh(t, last)
+        for t in range(PACK):
+            fetch_r1(t, last)
+        step_e(low, last)
+        step_hid(high, first)
+        woven_first = weave(0, first, False)
+        step_e(high, last)
+        for step in (step_g, step_m, step_x):
+            step(low, last)
+            step(high, last)
+        finish(0, first, woven_first, False)
+        step_hid(slice(0, PACK), last)
+        finish(1, last, weave(1, last, True), True)

@@ -102,8 +102,9 @@ def tile_picked_yretnx_max_p_kernel(
             nc.vector.tensor_copy(xs[o][:], xs_all[:, o, :].indirect(offs_sb[:]))
         nc.vector.tensor_copy(xw[0][:], xw_all[0][:].bitcast(U32).indirect(offs_sb[:]))
         deal_scales(early[:], w1s_raw, slice(0, 1))
-        for a in (0, half):
-            nc.vector.tensor_copy(xw[1][:, a : a + half], xw_all[1][:].bitcast(U32).indirect(offs_sb[:, a // 16 : (a + half) // 16]))
+        pieces = (slice(0, half), slice(half, S - TAIL), slice(S - TAIL, S))
+        for cols in pieces:
+            nc.vector.tensor_copy(xw[1][:, cols], xw_all[1][:].bitcast(U32).indirect(offs_sb[:, cols.start // 16 : cols.stop // 16]))
         late = keep.tile([P, PASSES, 2 * PACK - 1, P], U8, tag="slot1", align_bytes=64)
         deal_scales(late[:, :, : PACK - 1, :], w1s_raw, slice(1, PACK))
         deal_scales(late[:, :, PACK - 1 :, :], w2s_raw, slice(0, PACK))
@@ -138,7 +139,7 @@ def tile_picked_yretnx_max_p_kernel(
             nc.scalar.activation(out=tanh_ys[:, t, :], in_=ys[:], func=ACT.Tanh, scale=0.5)
 
         for t in range(PACK):
-            for cols in ((slice(0, half), slice(half, S)) if t == 0 else (slice(0, S),)):
+            for cols in pieces if t == 0 else (slice(0, S),):
                 y = product(w1w, w1s, t, cols)
                 nc.scalar.activation(out=tanh_y[t][:, cols], in_=y[:], func=ACT.Tanh)
                 nc.scalar.activation(out=inten[t][:, cols], in_=tanh_y[t][:, cols], func=ACT.Exp, scale=0.8)
@@ -224,23 +225,25 @@ def tile_picked_yretnx_max_p_kernel(
             nc.vector.quantize_mx(out=hid_w[:].bitcast(FP8X4), scales=hid_s[:], in_=woven[:])
             result = keep.tile([P, N // P, n], F32, name=f"result{c}")
             for m in range(N // P):
-                acc = psum.tile([P, n], F32, name=f"out{c}_{m}", tag=f"bank{1 + 2 * c + m}")
-                for a in range(0, n, half):
-                    b = min(a + half, n)
-                    nc.tensor.matmul_mx(
-                        out=acc[:, a:b],
-                        lhsT=w3w[:, 0, 2 * P * m : 2 * P * (m + 1)].bitcast(FP4X4),
-                        lhsT_scale=w3s[:, 0, P * m : P * (m + 1)],
-                        rhs=hid_w[:, a:b].bitcast(FP8X4),
-                        rhs_scale=hid_s[:, a:b],
-                        start=True,
-                        stop=True,
-                    )
+                acc = psum.tile([P, n], F32, name=f"out{c}_{m}", tag=f"bank{2 + 2 * c + m}")
+                nc.tensor.matmul_mx(
+                    out=acc[:],
+                    lhsT=w3w[:, 0, 2 * P * m : 2 * P * (m + 1)].bitcast(FP4X4),
+                    lhsT_scale=w3s[:, 0, P * m : P * (m + 1)],
+                    rhs=hid_w[:].bitcast(FP8X4),
+                    rhs_scale=hid_s[:],
+                    start=True,
+                    stop=True,
+                )
                 if share and m == 1:
                     nc.vector.tensor_copy(out=result[:, m, :], in_=acc[:])
                 else:
                     nc.scalar.copy(out=result[:, m, :], in_=acc[:])
-            nc.sync.dma_start(out=out[:, cols].rearrange("(m p) n -> p m n", p=P), in_=result[:])
+                if share:
+                    queue = nc.sync if m == 1 else nc.scalar
+                    queue.dma_start(out=out[P * m : P * (m + 1), cols], in_=result[:, m, :])
+            if not share:
+                nc.sync.dma_start(out=out[:, cols].rearrange("(m p) n -> p m n", p=P), in_=result[:])
 
         first, last = slice(0, S - TAIL), slice(S - TAIL, S)
         low, high = slice(0, 2), slice(2, 4)
@@ -273,11 +276,14 @@ def tile_picked_yretnx_max_p_kernel(
             fetch_r1(t, last)
         step_e(low, last)
         step_hid(high, first)
-        woven_first = weave(0, first, False)
+        woven = [weave(c, pieces[c], False) for c in range(2)]
         step_e(high, last)
-        for step in (step_g, step_m, step_x):
+        for step in (step_g, step_m):
             step(low, last)
             step(high, last)
-        finish(0, first, woven_first, False)
+        finish(0, pieces[0], woven[0], False)
+        step_x(low, last)
+        step_x(high, last)
         step_hid(slice(0, PACK), last)
-        finish(1, last, weave(1, last, True), True)
+        finish(1, pieces[1], woven[1], False)
+        finish(2, last, weave(2, last, True), True)

from contextlib import ExitStack

import concourse.mybir as mybir

K, T, S, N, H = 1024, 1024, 512, 256, 512
FLOPS = 2 * 2 * K * H * S + 2 * H * N * S

F32 = mybir.dt.float32
BF16 = mybir.dt.bfloat16
I32 = mybir.dt.int32
U32 = mybir.dt.uint32
U16 = mybir.dt.uint16
U8 = mybir.dt.uint8
FP8X4 = mybir.dt.float8_e4m3fn_x4
FP4X4 = mybir.dt.float4_e2m1fn_x4
ALU = mybir.AluOpType
ACT = mybir.ActivationFunctionType

P = 128
PACK = 4
PASSES = K // (P * PACK)
TAIL = 128


def tile_picked_yretnx_max_p_kernel(
    tc, x_words, x_scales, w1_words, w1_scales, w2_words, w2_scales, unit, w3_words, w3_scales, offs, s1, s2, far, out
):
    nc = tc.nc
    with ExitStack() as ctx:
        keep = ctx.enter_context(tc.tile_pool(name="keep", bufs=1))
        psum = ctx.enter_context(tc.psum_pool(name="psum", bufs=1))

        def load_scale_rows(tile, scales):
            for q in range(4):
                nc.sync.dma_start(
                    out=tile[32 * q : 32 * q + 4, :, :].bitcast(I32),
                    in_=scales[:, 4 * q : 4 * q + 4, :].rearrange("o r n -> r o n").bitcast(I32),
                )

        def load_list(name, source):
            tile = keep.tile([P, S // 16], U16, name=name)
            nc.sync.dma_start(tile[:], source)
            return tile

        def load_words(name, words):
            tile = keep.tile([P, words.shape[0], words.shape[2]], U8, name=name, align_bytes=64)
            nc.sync.dma_start(out=tile[:].bitcast(I32), in_=words.rearrange("o p n -> p o n").bitcast(I32))
            return tile

        xs_all = keep.tile([P, PASSES, T], U8, align_bytes=64)
        w1s_raw = keep.tile([P, PASSES, H], U8, align_bytes=64)
        w2s_raw = keep.tile([P, PASSES, H], U8, align_bytes=64)
        w3s = keep.tile([P, 1, N], U8, align_bytes=64)
        nc.gpsimd.memset(xs_all[:].bitcast(I32), 0)
        nc.vector.memset(w1s_raw[:].bitcast(I32), 0)
        nc.vector.memset(w2s_raw[:].bitcast(I32), 0)
        nc.vector.memset(w3s[:].bitcast(I32), 0)

        unit_sb = keep.tile([P, PACK], F32)
        nc.gpsimd.dma_start(out=unit_sb[:], in_=unit.rearrange("(p t) o -> p (t o)", t=PACK))

        offs_sb = load_list("offs_sb", offs)
        load_scale_rows(xs_all, x_scales)
        xw_all = [keep.tile([P, T], I32, name=f"xw_all{o}", tag=f"slot{o}", align_bytes=64) for o in range(PASSES)]
        nc.sync.dma_start(out=xw_all[0][:], in_=x_words[0].rearrange("p n t -> p (n t)").bitcast(I32))
        w1w_raw = load_words("w1w_raw", w1_words)
        load_scale_rows(w1s_raw, w1_scales)
        nc.sync.dma_start(out=xw_all[1][:], in_=x_words[1].rearrange("p n t -> p (n t)").bitcast(I32))
        w2w_raw = load_words("w2w_raw", w2_words)
        s1_sb = load_list("s1_sb", s1)
        load_scale_rows(w2s_raw, w2_scales)
        s2_sb = load_list("s2_sb", s2)
        far_sb = load_list("far_sb", far)
        w3w = load_words("w3w", w3_words)
        load_scale_rows(w3s, w3_scales)

        half_unit = keep.tile([P, PACK], F32)
        nc.scalar.activation(out=half_unit[:], in_=unit_sb[:], func=ACT.Copy, scale=0.5)

        def deal_words(name, raw):
            dealt = []
            for t in range(PACK):
                tile = keep.tile([P, PASSES, 2 * P], U8, name=f"{name}{t}", tag=f"{name}{t}", align_bytes=64)
                nc.scalar.copy(
                    out=tile[:].bitcast(U16),
                    in_=raw[:].bitcast(U16).rearrange("p o (m t) -> p o t m", t=PACK)[:, :, t, :],
                )
                dealt.append(tile)
            return dealt

        def deal_scales(dealt, raw, ts):
            nc.vector.tensor_copy(out=dealt, in_=raw[:].rearrange("p o (m t) -> p o t m", t=PACK)[:, :, ts, :])

        early = keep.tile([P, PASSES, 1, P], U8, align_bytes=64)
        w1w = deal_words("w1w", w1w_raw)
        w2w = deal_words("w2w", w2w_raw)

        half = S // 2
        xs = [keep.tile([P, S], U8, name=f"xs{o}", align_bytes=64) for o in range(PASSES)]
        xw = [keep.tile([P, S], U32, name=f"xw{o}", align_bytes=64) for o in range(PASSES)]
        for o in range(PASSES):
            nc.vector.tensor_copy(xs[o][:], xs_all[:, o, :].indirect(offs_sb[:]))
        nc.vector.tensor_copy(xw[0][:], xw_all[0][:].bitcast(U32).indirect(offs_sb[:]))
        deal_scales(early[:], w1s_raw, slice(0, 1))
        pieces = (slice(0, half), slice(half, S - TAIL), slice(S - TAIL, S))
        for cols in pieces:
            nc.vector.tensor_copy(xw[1][:, cols], xw_all[1][:].bitcast(U32).indirect(offs_sb[:, cols.start // 16 : cols.stop // 16]))
        late = keep.tile([P, PASSES, 2 * PACK - 1, P], U8, tag="slot1", align_bytes=64)
        deal_scales(late[:, :, : PACK - 1, :], w1s_raw, slice(1, PACK))
        deal_scales(late[:, :, PACK - 1 :, :], w2s_raw, slice(0, PACK))
        w1s = [[early[:, o, 0, :] if t == 0 else late[:, o, t - 1, :] for t in range(PACK)] for o in range(PASSES)]
        w2s = [[late[:, o, PACK - 1 + t, :] for t in range(PACK)] for o in range(PASSES)]

        banks = []

        def product(words, scales, t, cols):
            bank = len(banks) % 8
            acc = psum.tile([P, cols.stop - cols.start], F32, name=f"acc{len(banks)}", tag=f"bank{bank}")
            banks.append(acc)
            for o in range(PASSES):
                nc.tensor.matmul_mx(
                    out=acc[:],
                    lhsT=words[t][:, o, :].bitcast(FP4X4),
                    lhsT_scale=scales[o][t],
                    rhs=xw[o][:, cols].bitcast(FP8X4),
                    rhs_scale=xs[o][:, cols],
                    start=(o == 0),
                    stop=(o == PASSES - 1),
                )
            return acc

        both = [keep.tile([P, 2 * S], F32, name=f"both{t}") for t in range(PACK)]
        inten = [b[:, :S] for b in both]
        tanh_y = [b[:, S:] for b in both]
        tanh_ys = keep.tile([P, PACK, S], F32)

        def mixing_signal(t):
            ys = product(w2w, w2s, t, slice(0, S))
            nc.scalar.activation(out=tanh_ys[:, t, :], in_=ys[:], func=ACT.Tanh, scale=0.5)

        for t in range(PACK):
            for cols in pieces if t == 0 else (slice(0, S),):
                y = product(w1w, w1s, t, cols)
                nc.scalar.activation(out=tanh_y[t][:, cols], in_=y[:], func=ACT.Tanh)
                nc.scalar.activation(out=inten[t][:, cols], in_=tanh_y[t][:, cols], func=ACT.Exp, scale=0.8)
            if t > 0:
                mixing_signal(t - 1)
        mixing_signal(PACK - 1)

        near1 = keep.tile([P, PACK, S], F32)
        near_sum = [keep.tile([P, S], F32, name=f"near_sum{t}", tag=f"w2w{t + 1}" if t in (1, 2) else f"near_sum{t}", align_bytes=64) for t in range(PACK)]

        def fetch_near(t, cols):
            nc.vector.tensor_copy(near1[:, t, cols], both[t][:].indirect(s1_sb[:, cols.start // 16 : cols.stop // 16]))

        def add_near(t, cols):
            picked = both[t][:].indirect(s2_sb[:, cols.start // 16 : cols.stop // 16])
            nc.vector.tensor_tensor(near_sum[t][:, cols], picked, near1[:, t, cols], ALU.add)

        for step in (fetch_near, add_near):
            for cols in (slice(0, half), slice(half, S)):
                step(0, cols)
        fetch_near(1, slice(0, S))
        for t in range(1, PACK):
            if t + 1 < PACK:
                fetch_near(t + 1, slice(0, S))
            add_near(t, slice(0, S))
        logs = keep.tile([P, 3 * PACK * S], F32, tag="slot1", align_bytes=64)
        r1 = logs[:, : PACK * S].rearrange("p (t j) -> p t j", t=PACK)
        log_sur = logs[:, PACK * S : 2 * PACK * S].rearrange("p (t j) -> p t j", t=PACK)

        mix = logs[:, 2 * PACK * S :].rearrange("p (t j) -> p t j", t=PACK)
        r1_far = keep.tile([P, PACK, S], F32)
        hid = keep.tile([P, PACK, S], BF16)

        def far_slice(a, b):
            return far_sb[:, a // 16 : b // 16]

        def log_of_surround(t):
            nc.scalar.activation(out=log_sur[:, t, :], in_=near_sum[t][:], func=ACT.Ln, scale=0.5)

        def near_ratio(t):
            nc.vector.scalar_tensor_tensor(r1[:, t, :], tanh_y[t], 0.8, log_sur[:, t, :], ALU.mult, ALU.subtract)

        def fetch_tanh(t, cols):
            for a in range(cols.start, cols.stop, half):
                b = min(a + half, cols.stop)
                nc.scalar.activation(out=mix[:, t, a:b], in_=tanh_y[t].indirect(far_slice(a, b)), func=ACT.Copy)

        def fetch_r1(t, cols):
            window = logs[:, t * S : (t + 2) * S]
            nc.scalar.activation(out=r1_far[:, t, cols], in_=window.indirect(far_slice(cols.start, cols.stop)), func=ACT.Copy)

        def step_e(ts, cols):
            nc.vector.scalar_tensor_tensor(mix[:, ts, cols], mix[:, ts, cols], 0.8, log_sur[:, ts, cols], ALU.mult, ALU.subtract)

        def step_g(ts, cols):
            nc.vector.scalar_tensor_tensor(mix[:, ts, cols], tanh_ys[:, ts, cols], -1.0, mix[:, ts, cols], ALU.add, ALU.mult)

        def step_m(ts, cols):
            nc.vector.scalar_tensor_tensor(mix[:, ts, cols], r1[:, ts, cols], 2.0, mix[:, ts, cols], ALU.mult, ALU.add)

        def step_x(ts, cols):
            nc.vector.tensor_tensor(mix[:, ts, cols], mix[:, ts, cols], r1_far[:, ts, cols], ALU.max)

        def step_hid(ts, cols):
            for t in range(ts.start, ts.stop):
                nc.vector.scalar_tensor_tensor(hid[:, t, cols], mix[:, t, cols], half_unit[:, t : t + 1], inten[t][:, cols], ALU.mult, ALU.mult)

        def weave(c, cols, on_vector):
            n = cols.stop - cols.start
            woven = keep.tile([P, n * PACK], BF16, name=f"woven{c}", align_bytes=64)
            weave_out = woven[:].rearrange("p (c i t) -> p c t i", i=4, t=PACK)
            weave_in = hid[:, :, cols].rearrange("p t (c i) -> p c t i", i=4)
            if on_vector:
                nc.vector.tensor_copy(out=weave_out, in_=weave_in)
            else:
                nc.scalar.copy(out=weave_out, in_=weave_in)
            return woven

        def finish(c, cols, woven, share):
            n = cols.stop - cols.start
            hid_w = keep.tile([P, n], U32, name=f"hid_w{c}", align_bytes=64)
            hid_s = keep.tile([P, n], U8, name=f"hid_s{c}", align_bytes=64)
            nc.vector.quantize_mx(out=hid_w[:].bitcast(FP8X4), scales=hid_s[:], in_=woven[:])
            result = keep.tile([P, N // P, n], F32, name=f"result{c}")
            for m in range(N // P):
                acc = psum.tile([P, n], F32, name=f"out{c}_{m}", tag=f"bank{2 + 2 * c + m}")
                nc.tensor.matmul_mx(
                    out=acc[:],
                    lhsT=w3w[:, 0, 2 * P * m : 2 * P * (m + 1)].bitcast(FP4X4),
                    lhsT_scale=w3s[:, 0, P * m : P * (m + 1)],
                    rhs=hid_w[:].bitcast(FP8X4),
                    rhs_scale=hid_s[:],
                    start=True,
                    stop=True,
                )
                if share and m == 1:
                    nc.vector.tensor_copy(out=result[:, m, :], in_=acc[:])
                else:
                    nc.scalar.copy(out=result[:, m, :], in_=acc[:])
                if share:
                    queue = nc.sync if m == 1 else nc.scalar
                    queue.dma_start(out=out[P * m : P * (m + 1), cols], in_=result[:, m, :])
            if not share:
                nc.sync.dma_start(out=out[:, cols].rearrange("(m p) n -> p m n", p=P), in_=result[:])

        first, last = slice(0, S - TAIL), slice(S - TAIL, S)
        low, high = slice(0, 2), slice(2, 4)

        log_of_surround(0)
        log_of_surround(1)
        fetch_tanh(0, first)
        log_of_surround(2)
        fetch_tanh(1, first)
        log_of_surround(3)
        for t in range(3):
            near_ratio(t)
        step_e(low, first)
        near_ratio(3)
        fetch_tanh(2, first)
        fetch_tanh(3, first)
        for t in range(PACK):
            fetch_r1(t, first)
        step_g(low, first)
        step_e(high, first)
        step_m(low, first)
        step_g(high, first)
        step_x(low, first)
        step_m(high, first)
        step_hid(low, first)
        step_x(high, first)
        for t in range(PACK):
            fetch_tanh(t, last)
        for t in range(PACK):
            fetch_r1(t, last)
        step_e(low, last)
        step_hid(high, first)
        woven = [weave(c, pieces[c], False) for c in range(2)]
        step_e(high, last)
        for step in (step_g, step_m):
            step(low, last)
            step(high, last)
        finish(0, pieces[0], woven[0], False)
        step_x(low, last)
        step_x(high, last)
        step_hid(slice(0, PACK), last)
        finish(1, pieces[1], woven[1], False)
        finish(2, last, weave(2, last, True), True)
